import numpy as np
CORES = [7,63,135,191,263,319,391,447]
N = 8
def setup_inputs(rng):
    return {"x": rng.standard_normal((N, 128, 256), dtype=np.float32)}
def reference(x):
    b = 256 // N
    blocks = x.reshape(N, 128, N, b)
    return {"y": np.ascontiguousarray(blocks.transpose(2, 1, 0, 3)).reshape(N, 128, 256)}

@@ -1,0 +1,67 @@
+from concourse.bass import DstId, RemoteDMATransfer
+
+B = 32
+RELAY = 6
+
+SCRATCH = {
+    "s": ("sbuf", [128, 256], "float32"),
+    "land": ("sbuf", [128, 256], "float32"),
+    "rl": ("sbuf", [128, 64], "float32"),
+}
+SEMAPHORES = ["loaded", "own", "arr", "sent", "stored", "rarr", "rsent"]
+
+
+def _core(h, chip, lc=7):
+    return h * 128 + chip * 8 + lc
+
+
+def _blk(j):
+    return slice(j * B, (j + 1) * B)
+
+
+def _xfer(topo, src_core, dst_core, mask, sem, src, dst):
+    rid, pid = topo.addr(dst_core, src_core)
+    return RemoteDMATransfer(dst_ids=[DstId(rid=rid, pnc=pid)], dma_engine_mask=mask, remote_sem=sem, src=src, dst=dst)
+
+
+def rank_program(g, core, T, topo):
+    h, c, lc = topo.host(core), topo.chip(core), core % 8
+    if c not in (0, 7):
+        return
+    sem = T.sem
+    r = T.rank_of(core)
+    if r is None:
+        if lc != RELAY:
+            return
+        rs = T.rank_of(_core(3 - h, c))
+        g.wait_ge(sem.rarr, 8)
+        g.remote_dma_fused(
+            [_xfer(topo, core, _core(h ^ 1, dc), 0x0F << (4 * i), sem.arr, T.rl[:, _blk(i)], T.land[:, _blk(rs)])
+             for i, dc in enumerate((0, 7))],
+            local_sem=sem.rsent)
+        g.wait_ge(sem.rsent, 8)
+        return
+
+    m, k = h ^ 1, 3 - h
+    d = k ^ 1
+    cx = 7 - c
+    g.sync.dma_start(T.s[:], T.x[:]).then_inc(sem.loaded, 16)
+    g.sync.dma_start(T.land[:, _blk(r)], T.x[:, _blk(r)]).then_inc(sem.own, 16)
+
+    g.wait_ge(sem.loaded, 16)
+    rid, pid = topo.addr(_core(k, c, RELAY), core)
+    g.remote_dma(T.rl[:], T.s[:, 2 * d * B:(2 * d + 2) * B], sem.rarr, sem.sent, pid, rid, 0xFF)
+    four = [_core(k, cx), _core(k, c), _core(m, cx), _core(h, cx)]
+    g.remote_dma_fused(
+        [_xfer(topo, core, dst, 0x03 << (2 * i), sem.arr, T.s[:, _blk(T.rank_of(dst))], T.land[:, _blk(r)])
+         for i, dst in enumerate(four)],
+        local_sem=sem.sent)
+    dst = _core(m, c)
+    rid, pid = topo.addr(dst, core)
+    g.remote_dma(T.land[:, _blk(r)], T.s[:, _blk(T.rank_of(dst))], sem.arr, sem.sent, pid, rid, 0xFF)
+
+    g.sync.wait_ge(sem.own, 16)
+    g.sync.wait_ge(sem.arr, 24)
+    g.sync.dma_start(T.y[:], T.land[:]).then_inc(sem.stored, 16)
+    g.wait_ge(sem.sent, 24)
+    g.wait_ge(sem.stored, 16)

@@ -4,11 +4,11 @@ B = 32
 RELAY = 6
 
 SCRATCH = {
-    "s": ("sbuf", [128, 256], "float32"),
-    "land": ("sbuf", [128, 256], "float32"),
-    "rl": ("sbuf", [128, 64], "float32"),
+    "ds": ("dram", [8, 128, 32], "float32"),
+    "dl": ("dram", [8, 128, 32], "float32"),
+    "drl": ("dram", [2, 128, 32], "float32"),
 }
-SEMAPHORES = ["loaded", "own", "arr", "sent", "stored", "rarr", "rsent"]
+SEMAPHORES = ["la", "lb", "lc", "aa", "ab", "ac", "sent", "stored", "rarr", "rsent"]
 
 
 def _core(h, chip, lc=7):
@@ -36,7 +36,7 @@ def rank_program(g, core, T, topo):
         rs = T.rank_of(_core(3 - h, c))
         g.wait_ge(sem.rarr, 8)
         g.remote_dma_fused(
-            [_xfer(topo, core, _core(h ^ 1, dc), 0x0F << (4 * i), sem.arr, T.rl[:, _blk(i)], T.land[:, _blk(rs)])
+            [_xfer(topo, core, _core(h ^ 1, dc), 0x0F << (4 * i), sem.aa, T.drl[i], T.dl[rs])
              for i, dc in enumerate((0, 7))],
             local_sem=sem.rsent)
         g.wait_ge(sem.rsent, 8)
@@ -45,23 +45,53 @@ def rank_program(g, core, T, topo):
     m, k = h ^ 1, 3 - h
     d = k ^ 1
     cx = 7 - c
-    g.sync.dma_start(T.s[:], T.x[:]).then_inc(sem.loaded, 16)
-    g.sync.dma_start(T.land[:, _blk(r)], T.x[:, _blk(r)]).then_inc(sem.own, 16)
+    rk = T.rank_of
+    d0, d1 = rk(_core(d, 0)), rk(_core(d, 7))
+    kx, kc, sib = rk(_core(k, cx)), rk(_core(k, c)), rk(_core(h, cx))
+    mx, mc = rk(_core(m, cx)), rk(_core(m, c))
+    sy, sc = g.sync, g.scalar
 
-    g.wait_ge(sem.loaded, 16)
-    rid, pid = topo.addr(_core(k, c, RELAY), core)
-    g.remote_dma(T.rl[:], T.s[:, 2 * d * B:(2 * d + 2) * B], sem.rarr, sem.sent, pid, rid, 0xFF)
-    four = [_core(k, cx), _core(k, c), _core(m, cx), _core(h, cx)]
+    def load(q, j, s):
+        q.dma_start(T.ds[j], T.x[:, _blk(j)]).then_inc(s, 16)
+
+    def store(q, j):
+        q.dma_start(T.y[:, _blk(j)], T.dl[j]).then_inc(sem.stored, 16)
+
+    def send(j, mask, s):
+        return _xfer(topo, core, T.cores[j], mask, s, T.ds[j], T.dl[r])
+
+    load(sy, d0, sem.la)
+    load(sc, d1, sem.la)
+    load(sy, kx, sem.lb)
+    load(sc, kc, sem.lb)
+    load(sy, sib, sem.lb)
+    load(sc, mx, sem.lc)
+    load(sy, mc, sem.lc)
+    sc.dma_start(T.y[:, _blk(r)], T.x[:, _blk(r)]).then_inc(sem.stored, 16)
+
+    relay = _core(k, c, RELAY)
+    g.wait_ge(sem.la, 32)
     g.remote_dma_fused(
-        [_xfer(topo, core, dst, 0x03 << (2 * i), sem.arr, T.s[:, _blk(T.rank_of(dst))], T.land[:, _blk(r)])
-         for i, dst in enumerate(four)],
-        local_sem=sem.sent)
-    dst = _core(m, c)
-    rid, pid = topo.addr(dst, core)
-    g.remote_dma(T.land[:, _blk(r)], T.s[:, _blk(T.rank_of(dst))], sem.arr, sem.sent, pid, rid, 0xFF)
+        [_xfer(topo, core, relay, 0x0F, sem.rarr, T.ds[d0], T.drl[0]),
+         _xfer(topo, core, relay, 0xF0, sem.rarr, T.ds[d1], T.drl[1])], local_sem=sem.sent)
+    g.wait_ge(sem.lb, 48)
+    g.remote_dma_fused([send(kx, 0x0F, sem.ab), send(kc, 0x30, sem.ab), send(sib, 0xC0, sem.ab)], local_sem=sem.sent)
+    g.wait_ge(sem.lc, 32)
+    g.remote_dma_fused([send(mx, 0x0F, sem.ac), send(mc, 0xF0, sem.ac)], local_sem=sem.sent)
 
-    g.sync.wait_ge(sem.own, 16)
-    g.sync.wait_ge(sem.arr, 24)
-    g.sync.dma_start(T.y[:], T.land[:]).then_inc(sem.stored, 16)
+    for q in (sy, sc):
+        q.wait_ge(sem.ab, 8)
+    store(sy, kx)
+    store(sc, kc)
+    store(sy, sib)
+    for q in (sy, sc):
+        q.wait_ge(sem.ac, 8)
+    store(sc, mx)
+    store(sy, mc)
+    for q in (sy, sc):
+        q.wait_ge(sem.aa, 8)
+    store(sy, d0)
+    store(sc, d1)
+
     g.wait_ge(sem.sent, 24)
-    g.wait_ge(sem.stored, 16)
+    g.wait_ge(sem.stored, 128)

@@ -1,12 +1,13 @@
 from concourse.bass import DstId, RemoteDMATransfer
 
 B = 32
-RELAY = 6
+RELAY_C = 5
+RELAY_X = 6
 
 SCRATCH = {
     "ds": ("dram", [8, 128, 32], "float32"),
     "dl": ("dram", [8, 128, 32], "float32"),
-    "drl": ("dram", [2, 128, 32], "float32"),
+    "drl": ("dram", [128, 32], "float32"),
 }
 SEMAPHORES = ["la", "lb", "lc", "aa", "ab", "ac", "sent", "stored", "rarr", "rsent"]
 
@@ -31,14 +32,13 @@ def rank_program(g, core, T, topo):
     sem = T.sem
     r = T.rank_of(core)
     if r is None:
-        if lc != RELAY:
+        if lc not in (RELAY_C, RELAY_X):
             return
         rs = T.rank_of(_core(3 - h, c))
-        g.wait_ge(sem.rarr, 8)
-        g.remote_dma_fused(
-            [_xfer(topo, core, _core(h ^ 1, dc), 0x0F << (4 * i), sem.aa, T.drl[i], T.dl[rs])
-             for i, dc in enumerate((0, 7))],
-            local_sem=sem.rsent)
+        dst = _core(h ^ 1, c if lc == RELAY_C else 7 - c)
+        rid, pid = topo.addr(dst, core)
+        g.wait_ge(sem.rarr, 4)
+        g.remote_dma(T.dl[rs], T.drl[:], sem.aa, sem.rsent, pid, rid, 0xFF)
         g.wait_ge(sem.rsent, 8)
         return
 
@@ -46,7 +46,7 @@ def rank_program(g, core, T, topo):
     d = k ^ 1
     cx = 7 - c
     rk = T.rank_of
-    d0, d1 = rk(_core(d, 0)), rk(_core(d, 7))
+    dc, dx = rk(_core(d, c)), rk(_core(d, cx))
     kx, kc, sib = rk(_core(k, cx)), rk(_core(k, c)), rk(_core(h, cx))
     mx, mc = rk(_core(m, cx)), rk(_core(m, c))
     sy, sc = g.sync, g.scalar
@@ -60,38 +60,35 @@ def rank_program(g, core, T, topo):
     def send(j, mask, s):
         return _xfer(topo, core, T.cores[j], mask, s, T.ds[j], T.dl[r])
 
-    load(sy, d0, sem.la)
-    load(sc, d1, sem.la)
+    load(sy, dx, sem.la)
+    load(sc, dc, sem.la)
     load(sy, kx, sem.lb)
-    load(sc, kc, sem.lb)
+    load(sc, mx, sem.lb)
     load(sy, sib, sem.lb)
-    load(sc, mx, sem.lc)
+    load(sc, kc, sem.lc)
     load(sy, mc, sem.lc)
-    sc.dma_start(T.y[:, _blk(r)], T.x[:, _blk(r)]).then_inc(sem.stored, 16)
 
-    relay = _core(k, c, RELAY)
     g.wait_ge(sem.la, 32)
     g.remote_dma_fused(
-        [_xfer(topo, core, relay, 0x0F, sem.rarr, T.ds[d0], T.drl[0]),
-         _xfer(topo, core, relay, 0xF0, sem.rarr, T.ds[d1], T.drl[1])], local_sem=sem.sent)
+        [_xfer(topo, core, _core(k, c, RELAY_X), 0x0F, sem.rarr, T.ds[dx], T.drl[:]),
+         _xfer(topo, core, _core(k, c, RELAY_C), 0xF0, sem.rarr, T.ds[dc], T.drl[:])], local_sem=sem.sent)
     g.wait_ge(sem.lb, 48)
-    g.remote_dma_fused([send(kx, 0x0F, sem.ab), send(kc, 0x30, sem.ab), send(sib, 0xC0, sem.ab)], local_sem=sem.sent)
+    g.remote_dma_fused([send(kx, 0x0F, sem.ab), send(mx, 0x30, sem.ab), send(sib, 0xC0, sem.ab)], local_sem=sem.sent)
     g.wait_ge(sem.lc, 32)
-    g.remote_dma_fused([send(mx, 0x0F, sem.ac), send(mc, 0xF0, sem.ac)], local_sem=sem.sent)
+    g.remote_dma_fused([send(kc, 0x0F, sem.ac), send(mc, 0xF0, sem.ac)], local_sem=sem.sent)
 
-    for q in (sy, sc):
-        q.wait_ge(sem.ab, 8)
+    sc.wait_ge(sem.lc, 32)
+    sc.dma_start(T.y[:, _blk(r)], T.x[:, _blk(r)]).then_inc(sem.stored, 16)
+    sc.wait_ge(sem.aa, 16)
+    store(sc, dx)
+    store(sc, dc)
+    sy.wait_ge(sem.ab, 8)
     store(sy, kx)
-    store(sc, kc)
+    store(sy, mx)
     store(sy, sib)
-    for q in (sy, sc):
-        q.wait_ge(sem.ac, 8)
-    store(sc, mx)
+    sy.wait_ge(sem.ac, 8)
+    store(sy, kc)
     store(sy, mc)
-    for q in (sy, sc):
-        q.wait_ge(sem.aa, 8)
-    store(sy, d0)
-    store(sc, d1)
 
     g.wait_ge(sem.sent, 24)
     g.wait_ge(sem.stored, 128)

@@ -1,15 +1,15 @@
 from concourse.bass import DstId, RemoteDMATransfer
 
 B = 32
-RELAY_C = 5
-RELAY_X = 6
+RELAY_C = 6
+RELAY_X = 5
 
 SCRATCH = {
     "ds": ("dram", [8, 128, 32], "float32"),
     "dl": ("dram", [8, 128, 32], "float32"),
     "drl": ("dram", [128, 32], "float32"),
 }
-SEMAPHORES = ["la", "lb", "lc", "aa", "ab", "ac", "sent", "stored", "rarr", "rsent"]
+SEMAPHORES = ["la", "lb", "lc", "adc", "adx", "akx", "amx", "asib", "akc", "amc", "sent", "stored", "rarr", "rsent"]
 
 
 def _core(h, chip, lc=7):
@@ -34,11 +34,10 @@ def rank_program(g, core, T, topo):
     if r is None:
         if lc not in (RELAY_C, RELAY_X):
             return
-        rs = T.rank_of(_core(3 - h, c))
-        dst = _core(h ^ 1, c if lc == RELAY_C else 7 - c)
-        rid, pid = topo.addr(dst, core)
+        rs = T.rank_of(_core(h ^ 1, c if lc == RELAY_C else 7 - c))
+        rid, pid = topo.addr(_core(3 - h, c), core)
         g.wait_ge(sem.rarr, 4)
-        g.remote_dma(T.dl[rs], T.drl[:], sem.aa, sem.rsent, pid, rid, 0xFF)
+        g.remote_dma(T.dl[rs], T.drl[:], sem.adc if lc == RELAY_C else sem.adx, sem.rsent, pid, rid, 0xFF)
         g.wait_ge(sem.rsent, 8)
         return
 
@@ -54,7 +53,8 @@ def rank_program(g, core, T, topo):
     def load(q, j, s):
         q.dma_start(T.ds[j], T.x[:, _blk(j)]).then_inc(s, 16)
 
-    def store(q, j):
+    def store(q, j, s, n):
+        q.wait_ge(s, n)
         q.dma_start(T.y[:, _blk(j)], T.dl[j]).then_inc(sem.stored, 16)
 
     def send(j, mask, s):
@@ -70,25 +70,23 @@ def rank_program(g, core, T, topo):
 
     g.wait_ge(sem.la, 32)
     g.remote_dma_fused(
-        [_xfer(topo, core, _core(k, c, RELAY_X), 0x0F, sem.rarr, T.ds[dx], T.drl[:]),
-         _xfer(topo, core, _core(k, c, RELAY_C), 0xF0, sem.rarr, T.ds[dc], T.drl[:])], local_sem=sem.sent)
+        [_xfer(topo, core, _core(m, cx, RELAY_X), 0x0F, sem.rarr, T.ds[dx], T.drl[:]),
+         _xfer(topo, core, _core(m, c, RELAY_C), 0xF0, sem.rarr, T.ds[dc], T.drl[:])], local_sem=sem.sent)
     g.wait_ge(sem.lb, 48)
-    g.remote_dma_fused([send(kx, 0x0F, sem.ab), send(mx, 0x30, sem.ab), send(sib, 0xC0, sem.ab)], local_sem=sem.sent)
+    g.remote_dma_fused([send(kx, 0x0F, sem.akx), send(mx, 0x30, sem.amx), send(sib, 0xC0, sem.asib)],
+                       local_sem=sem.sent)
     g.wait_ge(sem.lc, 32)
-    g.remote_dma_fused([send(kc, 0x0F, sem.ac), send(mc, 0xF0, sem.ac)], local_sem=sem.sent)
+    g.remote_dma_fused([send(kc, 0x0F, sem.akc), send(mc, 0xF0, sem.amc)], local_sem=sem.sent)
 
     sc.wait_ge(sem.lc, 32)
     sc.dma_start(T.y[:, _blk(r)], T.x[:, _blk(r)]).then_inc(sem.stored, 16)
-    sc.wait_ge(sem.aa, 16)
-    store(sc, dx)
-    store(sc, dc)
-    sy.wait_ge(sem.ab, 8)
-    store(sy, kx)
-    store(sy, mx)
-    store(sy, sib)
-    sy.wait_ge(sem.ac, 8)
-    store(sy, kc)
-    store(sy, mc)
+    store(sc, dc, sem.adc, 8)
+    store(sc, dx, sem.adx, 8)
+    store(sy, sib, sem.asib, 2)
+    store(sy, mx, sem.amx, 2)
+    store(sy, kx, sem.akx, 4)
+    store(sy, mc, sem.amc, 4)
+    store(sy, kc, sem.akc, 4)
 
     g.wait_ge(sem.sent, 24)
     g.wait_ge(sem.stored, 128)

from concourse.bass import DstId, RemoteDMATransfer

B = 32
RELAY_C = 6
RELAY_X = 5

SCRATCH = {
    "ds": ("dram", [8, 128, 32], "float32"),
    "dl": ("dram", [8, 128, 32], "float32"),
    "drl": ("dram", [128, 32], "float32"),
}
SEMAPHORES = ["la", "lb", "lc", "adc", "adx", "akx", "amx", "asib", "akc", "amc", "sent", "stored", "rarr", "rsent"]


def _core(h, chip, lc=7):
    return h * 128 + chip * 8 + lc


def _blk(j):
    return slice(j * B, (j + 1) * B)


def _xfer(topo, src_core, dst_core, mask, sem, src, dst):
    rid, pid = topo.addr(dst_core, src_core)
    return RemoteDMATransfer(dst_ids=[DstId(rid=rid, pnc=pid)], dma_engine_mask=mask, remote_sem=sem, src=src, dst=dst)


def rank_program(g, core, T, topo):
    h, c, lc = topo.host(core), topo.chip(core), core % 8
    if c not in (0, 7):
        return
    sem = T.sem
    r = T.rank_of(core)
    if r is None:
        if lc not in (RELAY_C, RELAY_X):
            return
        rs = T.rank_of(_core(h ^ 1, c if lc == RELAY_C else 7 - c))
        rid, pid = topo.addr(_core(3 - h, c), core)
        g.wait_ge(sem.rarr, 4)
        g.remote_dma(T.dl[rs], T.drl[:], sem.adc if lc == RELAY_C else sem.adx, sem.rsent, pid, rid, 0xFF)
        g.wait_ge(sem.rsent, 8)
        return

    m, k = h ^ 1, 3 - h
    d = k ^ 1
    cx = 7 - c
    rk = T.rank_of
    dc, dx = rk(_core(d, c)), rk(_core(d, cx))
    kx, kc, sib = rk(_core(k, cx)), rk(_core(k, c)), rk(_core(h, cx))
    mx, mc = rk(_core(m, cx)), rk(_core(m, c))
    sy, sc = g.sync, g.scalar

    def load(q, j, s):
        q.dma_start(T.ds[j], T.x[:, _blk(j)]).then_inc(s, 16)

    def store(q, j, s, n):
        q.wait_ge(s, n)
        q.dma_start(T.y[:, _blk(j)], T.dl[j]).then_inc(sem.stored, 16)

    def send(j, mask, s):
        return _xfer(topo, core, T.cores[j], mask, s, T.ds[j], T.dl[r])

    load(sy, dx, sem.la)
    load(sc, dc, sem.la)
    load(sy, kx, sem.lb)
    load(sc, mx, sem.lb)
    load(sy, sib, sem.lb)
    load(sc, kc, sem.lc)
    load(sy, mc, sem.lc)

    g.wait_ge(sem.la, 32)
    g.remote_dma_fused(
        [_xfer(topo, core, _core(m, cx, RELAY_X), 0x0F, sem.rarr, T.ds[dx], T.drl[:]),
         _xfer(topo, core, _core(m, c, RELAY_C), 0xF0, sem.rarr, T.ds[dc], T.drl[:])], local_sem=sem.sent)
    g.wait_ge(sem.lb, 48)
    g.remote_dma_fused([send(kx, 0x0F, sem.akx), send(mx, 0x30, sem.amx), send(sib, 0xC0, sem.asib)],
                       local_sem=sem.sent)
    g.wait_ge(sem.lc, 32)
    g.remote_dma_fused([send(kc, 0x0F, sem.akc), send(mc, 0xF0, sem.amc)], local_sem=sem.sent)

    sc.wait_ge(sem.lc, 32)
    sc.dma_start(T.y[:, _blk(r)], T.x[:, _blk(r)]).then_inc(sem.stored, 16)
    store(sc, dc, sem.adc, 8)
    store(sc, dx, sem.adx, 8)
    store(sy, sib, sem.asib, 2)
    store(sy, mx, sem.amx, 2)
    store(sy, kx, sem.akx, 4)
    store(sy, mc, sem.amc, 4)
    store(sy, kc, sem.akc, 4)

    g.wait_ge(sem.sent, 24)
    g.wait_ge(sem.stored, 128)
